import numpy as np
import ml_dtypes


def mxq(x, axis, fmt="e4m3"):
    dtype, down = {"e4m3": (ml_dtypes.float8_e4m3fn, 7), "e5m2": (ml_dtypes.float8_e5m2, 14)}[fmt]
    v = np.moveaxis(np.asarray(x, np.float32).astype(ml_dtypes.bfloat16).astype(np.float64), axis, -1)
    blocks = v.reshape(v.shape[:-1] + (-1, 32))
    amax = np.abs(blocks).max(-1, keepdims=True)
    byte = np.maximum(np.where(amax > 0, np.frexp(amax)[1] - 1 + 127, 0) - down, 1)
    scale = np.exp2(byte - 127.0)
    codes = (blocks / scale).astype(np.float32).astype(dtype).astype(np.float64)
    return np.moveaxis((codes * scale).reshape(v.shape), -1, axis)


WIDE = False


def mx_kscale(k):
    if not WIDE:
        return np.ones(k)
    levels = np.array([30, -30])
    if k % 512:
        return np.exp2(np.random.permutation(np.resize(levels, k // 32))).repeat(32)
    a = np.empty((k // 512, 16))
    for p in range(k // 512):
        a[p, :8] = np.random.permutation(np.resize(levels, 8))
        for g in range(8):
            far = levels[np.abs(levels - a[p, g]) >= 10]
            a[p, g + 8] = far[np.random.randint(len(far))]
    return np.exp2(a.ravel()).repeat(32)


def f64(x):
    return np.asarray(x).astype(np.float64)


def striped(idx):
    return np.tile(np.asarray(idx).reshape(-1, 16).T, (8, 1)).astype(np.uint16)


def unstriped(offs):
    return offs[:16].T.reshape(-1).astype(np.int64)


E2M1 = np.array([0.0, 0.5, 1.0, 1.5, 2.0, 3.0, 4.0, 6.0, -0.0, -0.5, -1.0, -1.5, -2.0, -3.0, -4.0, -6.0])


def pack_weight(w, fmt):
    k, n = w.shape
    w = f64(np.asarray(w, np.float32).astype(ml_dtypes.bfloat16)).reshape(k // 32, 32, n)
    amax = np.abs(w).max(1)
    if fmt in ("e4m3", "e5m2"):
        byte = np.frexp(amax)[1] - 1 + 127 - (7 if fmt == "e4m3" else 14)
    else:
        mant, ex = np.frexp(amax / 6.0)
        byte = np.where(mant > 0.5, ex, ex - 1) + 127
    byte = np.clip(np.where(amax > 0, byte, 1), 1, 254)
    scaled = (w * np.exp2(127.0 - byte)[:, None, :]).reshape(k, n).astype(np.float32)
    by_word = np.ascontiguousarray(scaled.reshape(k // 512, 128, 4, n).transpose(0, 1, 3, 2))
    if fmt in ("e4m3", "e5m2"):
        words = by_word.astype(ml_dtypes.float8_e4m3fn if fmt == "e4m3" else ml_dtypes.float8_e5m2).view(np.uint8)
    else:
        c = by_word.astype(ml_dtypes.float4_e2m1fn).view(np.uint8) & 0xF
        words = (c[..., 0::2] | (c[..., 1::2] << 4)).reshape(k // 512, 128, 2 * n)
    return np.ascontiguousarray(words), np.ascontiguousarray(byte.astype(np.uint8).reshape(k // 512, 16, n))


def unpack_weight(words, scales, fmt):
    g, _, n = scales.shape
    words = np.ascontiguousarray(words).reshape(g, 128, n, -1)
    if fmt in ("e4m3", "e5m2"):
        vals = words.view(ml_dtypes.float8_e4m3fn if fmt == "e4m3" else ml_dtypes.float8_e5m2).astype(np.float64)
    else:
        nib = np.empty((g, 128, n, 4), np.uint8)
        nib[..., 0::2] = words & 0xF
        nib[..., 1::2] = words >> 4
        vals = E2M1[nib]
    vals = vals * np.repeat(np.exp2(scales.astype(np.float64) - 127.0), 8, axis=1)[..., None]
    return vals.transpose(0, 1, 3, 2).reshape(g * 512, n)


def bf(x):
    return np.asarray(x, np.float32).astype(ml_dtypes.bfloat16)


def planes(Y):
    r, m = Y.shape
    b = f64(bf(Y)).reshape(r // 32, 32, m)
    amax = np.abs(b).max(1)
    byte = np.clip(np.where(amax > 0, np.frexp(amax)[1] - 1 + 127 - 7, 1), 1, 254)
    codes = (b * np.exp2(127.0 - byte)[:, None, :]).reshape(r, m).astype(np.float32).astype(ml_dtypes.float8_e4m3fn).view(np.uint8)
    words = codes.reshape(r // 512, 128, 4, m).transpose(0, 1, 3, 2)
    return np.ascontiguousarray(words), np.ascontiguousarray(byte.astype(np.uint8).reshape(r // 512, 16, m))


K, T, J, R, F, V, N = 512, 512, 256, 512, 512, 512, 512


def setup_inputs():
    n = np.random.standard_normal
    idx = np.random.permutation(T)[:J]
    idx2 = np.random.permutation(V)[:J]
    fk = mx_kscale(K)
    fr = mx_kscale(R)
    ff = mx_kscale(F)
    wp = pack_weight(n((K, R)) * 1 / np.sqrt(K) * fk[:, None] * fr, "e4m3")
    sxp = pack_weight(n((F, J)) / ff[:, None], "e2m1")
    w2p = pack_weight(n((F, R)) * 1 / np.sqrt(F) * ff[:, None] * fr, "e5m2")
    wbp = pack_weight(n((R, N)) * 1 / np.sqrt(R) / fr[:, None], "e2m1")
    return {
        "xf": (n((K, T))).astype(np.float32),
        "fk": (np.random.uniform(0.5, 2.0, (K, 1)) / fk[:, None]).astype(np.float32),
        "w_words": wp[0],
        "w_scales": wp[1],
        "sx_words": sxp[0],
        "sx_scales": sxp[1],
        "w2_words": w2p[0],
        "w2_scales": w2p[1],
        "tb": (n((R, V)) * 0.7 * fr[:, None]).astype(np.float32),
        "wb_words": wbp[0],
        "wb_scales": wbp[1],
        "rs": (n((N, J))).astype(np.float32),
        "offs": striped(idx),
        "offs2": striped(idx2),
    }


def reference(xf, fk, w_words, w_scales, sx_words, sx_scales, w2_words, w2_scales, tb, wb_words, wb_scales, rs, offs, offs2):
    idx = unstriped(offs)
    idx2 = unstriped(offs2)
    wu = unpack_weight(w_words, w_scales, "e4m3")
    sxu = unpack_weight(sx_words, sx_scales, "e2m1")
    w2u = unpack_weight(w2_words, w2_scales, "e5m2")
    wbu = unpack_weight(wb_words, wb_scales, "e2m1")
    xg = f64(xf)[:, idx]
    x1 = np.pad(xg, ((0, 0), (1, 0)))[:, :J]
    u = (xg - 0.6 * x1) * f64(fk)
    uq = mxq(u, 0, "e4m3")
    a = wu.T @ uq + w2u.T @ sxu
    hid = np.maximum(a - f64(tb)[:, idx2], 0.0)
    hidq = mxq(hid, 0, "e5m2")
    p = wbu.T @ hidq
    p1 = np.pad(p, ((0, 0), (1, 0)))[:, :J]
    y = p - 0.7 * p1 + 0.5 * f64(rs)
    words, scales = planes(y)
    return y, words, scales

@@ -1,0 +1,187 @@
+from contextlib import ExitStack
+
+import concourse.mybir as mybir
+
+F32 = mybir.dt.float32
+BF16 = mybir.dt.bfloat16
+I32 = mybir.dt.int32
+U32 = mybir.dt.uint32
+U16 = mybir.dt.uint16
+U8 = mybir.dt.uint8
+E4M3 = mybir.dt.float8_e4m3fn_x4
+E5M2 = mybir.dt.float8_e5m2_x4
+E2M1 = mybir.dt.float4_e2m1fn_x4
+MULT = mybir.AluOpType.mult
+ADD = mybir.AluOpType.add
+SUB = mybir.AluOpType.subtract
+MAX = mybir.AluOpType.max
+COPY = mybir.ActivationFunctionType.Copy
+
+P = 128
+PACK = 4
+C = 512
+J = 256
+H = 128
+PAD = 8
+FLOPS = 3 * 2 * 512 * 512 * 256
+
+
+def tile_list_sum_steps_own_overtable_lagged_pl_kernel(
+    tc, xf, fk, w_words, w_scales, sx_words, sx_scales, w2_words, w2_scales, tb, wb_words, wb_scales, rs, offs, offs2,
+    out_0, out_1, out_2,
+):
+    nc = tc.nc
+    with ExitStack() as ctx:
+        sb = ctx.enter_context(tc.tile_pool(name="sb", bufs=1))
+        held = ctx.enter_context(tc.tile_pool(name="held", bufs=1))
+        ps = ctx.enter_context(tc.psum_pool(name="ps", bufs=1))
+
+        def tile(name, shape, dtype):
+            return sb.tile(shape, dtype, name=name, align_bytes=64)
+
+        def load_rows(dst, scales, width):
+            rows = scales[0].bitcast(I32).unsqueeze(0).broadcast_to([8, 16, width // 4])
+            nc.scalar.dma_start(out=dst.bitcast(I32), in_=rows)
+
+        def deal(copy, name, raw, dtype, view):
+            dealt = tile(name, raw.shape, dtype)
+            copy(out=dealt[:].bitcast(view).rearrange("p (t m) -> p m t", t=PACK),
+                 in_=raw[:].bitcast(view).rearrange("p (m t) -> p m t", t=PACK))
+            return dealt
+
+        def walk_planes(ap):
+            return ap.rearrange("p t (c i) -> p c t i", i=4)
+
+        def walk_words(ap):
+            return ap.rearrange("p (c i t) -> p c t i", i=4, t=PACK)
+
+        xf_v = xf.rearrange("(p t) c -> p t c", t=PACK)
+        tb_v = tb.rearrange("(p t) c -> p t c", t=PACK)
+
+        offs_t = tile("offs_t", [P, J // 16], U16)
+        nc.sync.dma_start(offs_t[:], offs)
+        fk_t = tile("fk_t", [P, PACK], F32)
+        nc.sync.dma_start(out=fk_t[:], in_=fk.rearrange("(p t) o -> p (t o)", t=PACK))
+        x01 = tile("x01", [P, 2, C], F32)
+        nc.sync.dma_start(out=x01[:], in_=xf_v[:, 0:2, :])
+        staged = held.tile([P, 3 * C], U8, name="staged", offset=3072)
+        planes = tile("planes", [P, 3 * C + J], U8)
+        for a, scales in enumerate((w2_scales, w_scales, wb_scales)):
+            load_rows(staged[:, a * C : (a + 1) * C], scales, C)
+        load_rows(planes[:, 3 * C :], sx_scales, J)
+        x2 = tile("x2", [P, C], F32)
+        nc.sync.dma_start(out=x2[:], in_=xf_v[:, 2, :])
+        x3 = tile("x3", [P, C], F32)
+        nc.sync.dma_start(out=x3[:], in_=xf_v[:, 3, :])
+        offs2_t = tile("offs2_t", [P, J // 16], U16)
+        nc.sync.dma_start(offs2_t[:], offs2)
+        w2_raw = tile("w2_raw", [P, C], U32)
+        nc.sync.dma_start(out=w2_raw[:].bitcast(I32), in_=w2_words[0].rearrange("p n t -> p (n t)").bitcast(I32))
+        w_raw = tile("w_raw", [P, C], U32)
+        nc.sync.dma_start(out=w_raw[:].bitcast(I32), in_=w_words[0].rearrange("p n t -> p (n t)").bitcast(I32))
+        sx_t = tile("sx_t", [P, 2 * J], U8)
+        nc.sync.dma_start(out=sx_t[:].bitcast(I32), in_=sx_words[0].bitcast(I32))
+
+        g = tile("g", [P, PACK, PAD + J], F32)
+        nc.vector.memset(g[:, :, 0:PAD], 0.0)
+        fk_wide = sb.tile([P, 2, J], F32, name="fk_wide", tag="fk_wide_then_rs", align_bytes=64)
+        nc.vector.tensor_copy(out=fk_wide[:], in_=fk_t[:, 2:4].unsqueeze(2).broadcast_to([P, 2, J]))
+        nc.vector.tensor_copy(out=planes[:, 0 : 3 * C].rearrange("p (a t m) -> p a m t", a=3, t=PACK),
+                              in_=staged[:].rearrange("p (a m t) -> p a m t", a=3, t=PACK))
+        for q in range(1, 4):
+            nc.sync.dma_start(out=planes[32 * q : 32 * q + 4, :].bitcast(I32), in_=planes[4 * q : 4 * q + 4, :].bitcast(I32))
+        tb01 = held.tile([P, 2, C], F32, name="tb01", offset=0)
+        nc.sync.dma_start(out=tb01[:], in_=tb_v[:, 0:2, :])
+        tb23 = held.tile([P, 2, C], F32, name="tb23", offset=4096)
+        nc.sync.dma_start(out=tb23[:], in_=tb_v[:, 2:4, :])
+        w2s, ws, wbs, sxs = planes[:, 0:C], planes[:, C : 2 * C], planes[:, 2 * C : 3 * C], planes[:, 3 * C :]
+
+        picked = sb.tile([P, 2, J], F32, name="picked", tag="picked_then_wb", align_bytes=64)
+        for t in range(2):
+            nc.scalar.activation(picked[:, t, :], x01[:, t, :].indirect(offs_t[:]), COPY)
+            nc.scalar.activation(g[:, t, PAD:], picked[:, t, :], COPY, scale=fk_t[:, t : t + 1])
+        for t, x in ((2, x2), (3, x3)):
+            nc.vector.tensor_tensor(g[:, t, PAD:], x[:].indirect(offs_t[:]), fk_wide[:, t - 2, :], MULT)
+
+        wb_raw = sb.tile([P, 2 * C], U8, name="wb_raw", tag="picked_then_wb", align_bytes=64)
+        nc.sync.dma_start(out=wb_raw[:].bitcast(I32), in_=wb_words[0].bitcast(I32))
+        rs_t = sb.tile([P, PACK, J], F32, name="rs_t", tag="fk_wide_then_rs", align_bytes=64)
+        nc.sync.dma_start(out=rs_t[:], in_=rs.rearrange("(p t) j -> p t j", t=PACK))
+        w2d = deal(nc.scalar.copy, "w2d", w2_raw, U32, U32)
+        wd = deal(nc.scalar.copy, "wd", w_raw, U32, U32)
+
+        a_bank = [ps.tile([P, PACK, H], F32, name="a_bank%d" % h) for h in range(2)]
+        p_bank = [ps.tile([P, PACK, H], F32, name="p_bank%d" % h) for h in range(2)]
+        for h in range(2):
+            for t in range(PACK):
+                nc.tensor.matmul_mx(out=a_bank[h][:, t, :], lhsT=w2d[:, t * P : (t + 1) * P].bitcast(E5M2),
+                                    lhsT_scale=w2s[:, t * P : (t + 1) * P],
+                                    rhs=sx_t[:, 2 * h * H : 2 * (h + 1) * H].bitcast(E2M1),
+                                    rhs_scale=sxs[:, h * H : (h + 1) * H], start=(t == 0), stop=False)
+
+        ub = [tile("ub%d" % h, [P, H, PACK], BF16) for h in range(2)]
+        uq = [tile("uq%d" % h, [P, H], U32) for h in range(2)]
+        us = [tile("us%d" % h, [P, H], U8) for h in range(2)]
+        for h in range(2):
+            now = g[:, :, PAD + h * H : PAD + (h + 1) * H].rearrange("p t c -> p c t")
+            before = g[:, :, PAD - 1 + h * H : PAD - 1 + (h + 1) * H].rearrange("p t c -> p c t")
+            nc.vector.scalar_tensor_tensor(ub[h][:], before, -0.6, now, MULT, ADD)
+        for h in range(2):
+            nc.vector.quantize_mx(out=uq[h][:].bitcast(E4M3), scales=us[h][:], in_=ub[h][:].rearrange("p c t -> p (c t)"))
+        for h in range(2):
+            for t in range(PACK):
+                nc.tensor.matmul_mx(out=a_bank[h][:, t, :], lhsT=wd[:, t * P : (t + 1) * P].bitcast(E4M3),
+                                    lhsT_scale=ws[:, t * P : (t + 1) * P], rhs=uq[h][:].bitcast(E4M3),
+                                    rhs_scale=us[h][:], start=False, stop=(t == PACK - 1))
+
+        tg = [tile("tg%d" % h, [P, PACK, H], F32) for h in range(2)]
+        half = [offs2_t[:, 0:8], offs2_t[:, 8:16]]
+        for t in range(2):
+            for h in range(2):
+                nc.scalar.activation(tg[h][:, t, :], tb01[:, t, :].indirect(half[h]), COPY)
+        nc.vector.tensor_copy(tg[0][:, 3, :], tb23[:, 1, :].indirect(half[0]))
+        nc.scalar.activation(tg[0][:, 2, :], tb23[:, 0, :].indirect(half[0]), COPY)
+        nc.scalar.activation(tg[1][:, 2, :], tb23[:, 0, :].indirect(half[1]), COPY)
+        nc.scalar.activation(tg[1][:, 3, :], tb23[:, 1, :].indirect(half[1]), COPY)
+        wbd = deal(nc.scalar.copy, "wbd", wb_raw, U8, U16)
+
+        db = [tile("db%d" % h, [P, H * PACK], BF16) for h in range(2)]
+        hb = [tile("hb%d" % h, [P, H * PACK], BF16) for h in range(2)]
+        hq = [tile("hq%d" % h, [P, H], U32) for h in range(2)]
+        hs = [tile("hs%d" % h, [P, H], U8) for h in range(2)]
+        for h in range(2):
+            nc.vector.tensor_tensor(walk_words(db[h][:]), walk_planes(a_bank[h][:]), walk_planes(tg[h][:]), SUB)
+        for h in range(2):
+            nc.vector.tensor_scalar(hb[h][:], db[h][:], 0.0, None, MAX)
+        for h in range(2):
+            nc.vector.quantize_mx(out=hq[h][:].bitcast(E5M2), scales=hs[h][:], in_=hb[h][:])
+        for h in range(2):
+            for t in range(PACK):
+                nc.tensor.matmul_mx(out=p_bank[h][:, t, :], lhsT=wbd[:, 2 * t * P : 2 * (t + 1) * P].bitcast(E2M1),
+                                    lhsT_scale=wbs[:, t * P : (t + 1) * P], rhs=hq[h][:].bitcast(E5M2),
+                                    rhs_scale=hs[h][:], start=True, stop=True)
+
+        lag = tile("lag", [P, PACK, J], F32)
+        ratio = 0.5 / -0.7
+        nc.vector.tensor_scalar(lag[:, :, 0:1], rs_t[:, :, 0:1], ratio, None, MULT)
+        y = [tile("y%d" % h, [P, PACK, H], F32) for h in range(2)]
+        yb = [tile("yb%d" % h, [P, H * PACK], BF16) for h in range(2)]
+        yq = [tile("yq%d" % h, [P, H], U32) for h in range(2)]
+        ys = tile("ys", [P, J], U8)
+        out_v = out_0.rearrange("(p t) j -> p t j", t=PACK)
+        words_v = out_1[0].rearrange("p c t -> p (c t)").bitcast(I32)
+        for h in range(2):
+            n = min(H, J - 1 - h * H)
+            cols = slice(h * H + 1, h * H + 1 + n)
+            nc.vector.scalar_tensor_tensor(lag[:, :, cols], rs_t[:, :, cols], ratio, p_bank[h][:, :, 0:n], MULT, ADD)
+        for h in range(2):
+            nc.vector.scalar_tensor_tensor(y[h][:], lag[:, :, h * H : (h + 1) * H], -0.7, p_bank[h][:], MULT, ADD)
+            nc.sync.dma_start(out=out_v[:, :, h * H : (h + 1) * H], in_=y[h][:])
+        nc.scalar.copy(out=walk_words(yb[0][:]), in_=walk_planes(y[0][:]))
+        nc.vector.tensor_copy(out=walk_words(yb[1][:]), in_=walk_planes(y[1][:]))
+        for h in range(2):
+            nc.vector.quantize_mx(out=yq[h][:].bitcast(E4M3), scales=ys[:, h * H : (h + 1) * H], in_=yb[h][:])
+            nc.sync.dma_start(out=words_v[:, h * H : (h + 1) * H], in_=yq[h][:].bitcast(I32))
+        for q in range(4):
+            queue = nc.scalar if q % 2 else nc.sync
+            queue.dma_start(out=out_2[0].bitcast(I32)[4 * q : 4 * q + 4, :], in_=ys[32 * q : 32 * q + 4, :].bitcast(I32))

@@ -17,6 +17,7 @@ SUB = mybir.AluOpType.subtract
 MAX = mybir.AluOpType.max
 COPY = mybir.ActivationFunctionType.Copy
 
+RELU = mybir.ActivationFunctionType.Relu
 P = 128
 PACK = 4
 C = 512
@@ -39,9 +40,12 @@ def tile_list_sum_steps_own_overtable_lagged_pl_kernel(
         def tile(name, shape, dtype):
             return sb.tile(shape, dtype, name=name, align_bytes=64)
 
-        def load_rows(dst, scales, width):
-            rows = scales[0].bitcast(I32).unsqueeze(0).broadcast_to([8, 16, width // 4])
-            nc.scalar.dma_start(out=dst.bitcast(I32), in_=rows)
+        def placed(name, shape, dtype, offset):
+            return held.tile(shape, dtype, name=name, offset=offset, align_bytes=64)
+
+        def load_rows(queue, dst, scales, width):
+            rows = scales[0].bitcast(I32).unsqueeze(0).broadcast_to([2, 16, width // 4])
+            queue.dma_start(out=dst.bitcast(I32), in_=rows)
 
         def deal(copy, name, raw, dtype, view):
             dealt = tile(name, raw.shape, dtype)
@@ -62,63 +66,59 @@ def tile_list_sum_steps_own_overtable_lagged_pl_kernel(
         nc.sync.dma_start(offs_t[:], offs)
         fk_t = tile("fk_t", [P, PACK], F32)
         nc.sync.dma_start(out=fk_t[:], in_=fk.rearrange("(p t) o -> p (t o)", t=PACK))
+        staged = placed("staged", [P, 3 * C + J], U8, 4096)
+        planes = tile("planes", [P, 3 * C + J], U8)
+        load_rows(nc.sync, staged[0:32, 3 * C :], sx_scales, J)
+        for a, scales in enumerate((w2_scales, w_scales, wb_scales)):
+            load_rows(nc.scalar, staged[0:32, a * C : (a + 1) * C], scales, C)
+        nc.vector.memset(staged[32:64, :].bitcast(I32), 0)
+        nc.vector.memset(staged[64:128, :].bitcast(I32), 0)
         x01 = tile("x01", [P, 2, C], F32)
         nc.sync.dma_start(out=x01[:], in_=xf_v[:, 0:2, :])
-        staged = held.tile([P, 3 * C], U8, name="staged", offset=3072)
-        planes = tile("planes", [P, 3 * C + J], U8)
-        for a, scales in enumerate((w2_scales, w_scales, wb_scales)):
-            load_rows(staged[:, a * C : (a + 1) * C], scales, C)
-        load_rows(planes[:, 3 * C :], sx_scales, J)
-        x2 = tile("x2", [P, C], F32)
-        nc.sync.dma_start(out=x2[:], in_=xf_v[:, 2, :])
-        x3 = tile("x3", [P, C], F32)
-        nc.sync.dma_start(out=x3[:], in_=xf_v[:, 3, :])
-        offs2_t = tile("offs2_t", [P, J // 16], U16)
-        nc.sync.dma_start(offs2_t[:], offs2)
-        w2_raw = tile("w2_raw", [P, C], U32)
+        x23 = tile("x23", [P, 2, C], F32)
+        nc.sync.dma_start(out=x23[:], in_=xf_v[:, 2:4, :])
+        w2_raw = placed("w2_raw", [P, C], U32, 8192)
         nc.sync.dma_start(out=w2_raw[:].bitcast(I32), in_=w2_words[0].rearrange("p n t -> p (n t)").bitcast(I32))
-        w_raw = tile("w_raw", [P, C], U32)
+        w_raw = placed("w_raw", [P, C], U32, 10240)
         nc.sync.dma_start(out=w_raw[:].bitcast(I32), in_=w_words[0].rearrange("p n t -> p (n t)").bitcast(I32))
         sx_t = tile("sx_t", [P, 2 * J], U8)
-        nc.sync.dma_start(out=sx_t[:].bitcast(I32), in_=sx_words[0].bitcast(I32))
+        nc.gpsimd.dma_start(out=sx_t[:].bitcast(I32), in_=sx_words[0].bitcast(I32))
+        offs2_t = tile("offs2_t", [P, J // 16], U16)
+        nc.sync.dma_start(offs2_t[:], offs2)
+        tb01 = tile("tb01", [P, 2, C], F32)
+        nc.sync.dma_start(out=tb01[:], in_=tb_v[:, 0:2, :])
 
         g = tile("g", [P, PACK, PAD + J], F32)
-        nc.vector.memset(g[:, :, 0:PAD], 0.0)
-        fk_wide = sb.tile([P, 2, J], F32, name="fk_wide", tag="fk_wide_then_rs", align_bytes=64)
-        nc.vector.tensor_copy(out=fk_wide[:], in_=fk_t[:, 2:4].unsqueeze(2).broadcast_to([P, 2, J]))
-        nc.vector.tensor_copy(out=planes[:, 0 : 3 * C].rearrange("p (a t m) -> p a m t", a=3, t=PACK),
-                              in_=staged[:].rearrange("p (a m t) -> p a m t", a=3, t=PACK))
+        zeros = tile("zeros", [P, PACK, 1], F32)
+        nc.vector.memset(zeros[:], 0.0)
+        nc.scalar.activation(g[:, :, PAD - 1 : PAD], zeros[:], COPY)
+        nc.vector.tensor_copy(out=planes[:, 3 * C :].bitcast(I32), in_=staged[:, 3 * C :].bitcast(I32))
+        nc.vector.tensor_copy(out=planes[:, 0 : 3 * C].rearrange("p (a t m i) -> p a m t i", a=3, t=PACK, i=16),
+                              in_=staged[:, 0 : 3 * C].rearrange("p (a m i t) -> p a m t i", a=3, t=PACK, i=16))
         for q in range(1, 4):
             nc.sync.dma_start(out=planes[32 * q : 32 * q + 4, :].bitcast(I32), in_=planes[4 * q : 4 * q + 4, :].bitcast(I32))
-        tb01 = held.tile([P, 2, C], F32, name="tb01", offset=0)
-        nc.sync.dma_start(out=tb01[:], in_=tb_v[:, 0:2, :])
-        tb23 = held.tile([P, 2, C], F32, name="tb23", offset=4096)
-        nc.sync.dma_start(out=tb23[:], in_=tb_v[:, 2:4, :])
+        tb2 = placed("tb2", [P, C], F32, 3072)
+        nc.sync.dma_start(out=tb2[:], in_=tb_v[:, 2, :])
+        tb3 = placed("tb3", [P, C], F32, 5120)
+        nc.sync.dma_start(out=tb3[:], in_=tb_v[:, 3, :])
         w2s, ws, wbs, sxs = planes[:, 0:C], planes[:, C : 2 * C], planes[:, 2 * C : 3 * C], planes[:, 3 * C :]
 
-        picked = sb.tile([P, 2, J], F32, name="picked", tag="picked_then_wb", align_bytes=64)
-        for t in range(2):
-            nc.scalar.activation(picked[:, t, :], x01[:, t, :].indirect(offs_t[:]), COPY)
-            nc.scalar.activation(g[:, t, PAD:], picked[:, t, :], COPY, scale=fk_t[:, t : t + 1])
-        for t, x in ((2, x2), (3, x3)):
-            nc.vector.tensor_tensor(g[:, t, PAD:], x[:].indirect(offs_t[:]), fk_wide[:, t - 2, :], MULT)
+        picked = [tile("picked%d" % t, [P, J], F32) for t in range(PACK)]
+        for t, x in ((0, x01), (2, x23)):
+            nc.scalar.activation(picked[t][:], x[:, 0, :].indirect(offs_t[:]), COPY)
+            nc.scalar.activation(g[:, t, PAD:], picked[t][:], COPY, scale=fk_t[:, t : t + 1])
+            nc.vector.tensor_copy(picked[t + 1][:], x[:, 1, :].indirect(offs_t[:]))
+            nc.vector.tensor_scalar(g[:, t + 1, PAD:], picked[t + 1][:], fk_t[:, t + 1 : t + 2], None, MULT)
 
-        wb_raw = sb.tile([P, 2 * C], U8, name="wb_raw", tag="picked_then_wb", align_bytes=64)
-        nc.sync.dma_start(out=wb_raw[:].bitcast(I32), in_=wb_words[0].bitcast(I32))
-        rs_t = sb.tile([P, PACK, J], F32, name="rs_t", tag="fk_wide_then_rs", align_bytes=64)
-        nc.sync.dma_start(out=rs_t[:], in_=rs.rearrange("(p t) j -> p t j", t=PACK))
         w2d = deal(nc.scalar.copy, "w2d", w2_raw, U32, U32)
+        wb_raw = placed("wb_raw", [P, 2 * C], U8, 8192)
+        nc.sync.dma_start(out=wb_raw[:].bitcast(I32), in_=wb_words[0].bitcast(I32))
         wd = deal(nc.scalar.copy, "wd", w_raw, U32, U32)
+        rs_t = placed("rs_t", [P, PACK, J], F32, 10240)
+        nc.sync.dma_start(out=rs_t[:], in_=rs.rearrange("(p t) j -> p t j", t=PACK))
 
         a_bank = [ps.tile([P, PACK, H], F32, name="a_bank%d" % h) for h in range(2)]
         p_bank = [ps.tile([P, PACK, H], F32, name="p_bank%d" % h) for h in range(2)]
-        for h in range(2):
-            for t in range(PACK):
-                nc.tensor.matmul_mx(out=a_bank[h][:, t, :], lhsT=w2d[:, t * P : (t + 1) * P].bitcast(E5M2),
-                                    lhsT_scale=w2s[:, t * P : (t + 1) * P],
-                                    rhs=sx_t[:, 2 * h * H : 2 * (h + 1) * H].bitcast(E2M1),
-                                    rhs_scale=sxs[:, h * H : (h + 1) * H], start=(t == 0), stop=False)
-
         ub = [tile("ub%d" % h, [P, H, PACK], BF16) for h in range(2)]
         uq = [tile("uq%d" % h, [P, H], U32) for h in range(2)]
         us = [tile("us%d" % h, [P, H], U8) for h in range(2)]
@@ -130,19 +130,21 @@ def tile_list_sum_steps_own_overtable_lagged_pl_kernel(
             nc.vector.quantize_mx(out=uq[h][:].bitcast(E4M3), scales=us[h][:], in_=ub[h][:].rearrange("p c t -> p (c t)"))
         for h in range(2):
             for t in range(PACK):
+                nc.tensor.matmul_mx(out=a_bank[h][:, t, :], lhsT=w2d[:, t * P : (t + 1) * P].bitcast(E5M2),
+                                    lhsT_scale=w2s[:, t * P : (t + 1) * P],
+                                    rhs=sx_t[:, 2 * h * H : 2 * (h + 1) * H].bitcast(E2M1),
+                                    rhs_scale=sxs[:, h * H : (h + 1) * H], start=(t == 0), stop=False)
+            for t in range(PACK):
                 nc.tensor.matmul_mx(out=a_bank[h][:, t, :], lhsT=wd[:, t * P : (t + 1) * P].bitcast(E4M3),
                                     lhsT_scale=ws[:, t * P : (t + 1) * P], rhs=uq[h][:].bitcast(E4M3),
                                     rhs_scale=us[h][:], start=False, stop=(t == PACK - 1))
 
-        tg = [tile("tg%d" % h, [P, PACK, H], F32) for h in range(2)]
-        half = [offs2_t[:, 0:8], offs2_t[:, 8:16]]
-        for t in range(2):
-            for h in range(2):
-                nc.scalar.activation(tg[h][:, t, :], tb01[:, t, :].indirect(half[h]), COPY)
-        nc.vector.tensor_copy(tg[0][:, 3, :], tb23[:, 1, :].indirect(half[0]))
-        nc.scalar.activation(tg[0][:, 2, :], tb23[:, 0, :].indirect(half[0]), COPY)
-        nc.scalar.activation(tg[1][:, 2, :], tb23[:, 0, :].indirect(half[1]), COPY)
-        nc.scalar.activation(tg[1][:, 3, :], tb23[:, 1, :].indirect(half[1]), COPY)
+        tg = tile("tg", [P, PACK, J], F32)
+        nc.scalar.activation(tg[:, 0, :], tb01[:, 0, :].indirect(offs2_t[:]), COPY)
+        nc.vector.tensor_copy(tg[:, 1, :], tb01[:, 1, :].indirect(offs2_t[:]))
+        nc.scalar.activation(tg[:, 2, :], tb2[:].indirect(offs2_t[:]), COPY)
+        nc.vector.tensor_copy(tg[:, 3, 0:H], tb3[:].indirect(offs2_t[:, 0:8]))
+        nc.scalar.activation(tg[:, 3, H:J], tb3[:].indirect(offs2_t[:, 8:16]), COPY)
         wbd = deal(nc.scalar.copy, "wbd", wb_raw, U8, U16)
 
         db = [tile("db%d" % h, [P, H * PACK], BF16) for h in range(2)]
@@ -150,9 +152,9 @@ def tile_list_sum_steps_own_overtable_lagged_pl_kernel(
         hq = [tile("hq%d" % h, [P, H], U32) for h in range(2)]
         hs = [tile("hs%d" % h, [P, H], U8) for h in range(2)]
         for h in range(2):
-            nc.vector.tensor_tensor(walk_words(db[h][:]), walk_planes(a_bank[h][:]), walk_planes(tg[h][:]), SUB)
-        for h in range(2):
-            nc.vector.tensor_scalar(hb[h][:], db[h][:], 0.0, None, MAX)
+            nc.vector.tensor_tensor(walk_words(db[h][:]), walk_planes(a_bank[h][:]), walk_planes(tg[:, :, h * H : (h + 1) * H]), SUB)
+        nc.scalar.activation(hb[0][:], db[0][:], RELU)
+        nc.vector.tensor_scalar(hb[1][:], db[1][:], 0.0, None, MAX)
         for h in range(2):
             nc.vector.quantize_mx(out=hq[h][:].bitcast(E5M2), scales=hs[h][:], in_=hb[h][:])
         for h in range(2):

@@ -47,17 +47,17 @@ def tile_list_sum_steps_own_overtable_lagged_pl_kernel(
             rows = scales[0].bitcast(I32).unsqueeze(0).broadcast_to([2, 16, width // 4])
             queue.dma_start(out=dst.bitcast(I32), in_=rows)
 
-        def deal(copy, name, raw, dtype, view):
+        def deal(copy, name, raw, dtype, view, run):
             dealt = tile(name, raw.shape, dtype)
-            copy(out=dealt[:].bitcast(view).rearrange("p (t m) -> p m t", t=PACK),
-                 in_=raw[:].bitcast(view).rearrange("p (m t) -> p m t", t=PACK))
+            copy(out=dealt[:].bitcast(view).rearrange("p (t m i) -> p m t i", t=PACK, i=run),
+                 in_=raw[:].bitcast(view).rearrange("p (m i t) -> p m t i", t=PACK, i=run))
             return dealt
 
         def walk_planes(ap):
-            return ap.rearrange("p t (c i) -> p c t i", i=4)
+            return ap.rearrange("p t (c i) -> p c t i", i=2)
 
         def walk_words(ap):
-            return ap.rearrange("p (c i t) -> p c t i", i=4, t=PACK)
+            return ap.rearrange("p (c i t) -> p c t i", i=2, t=PACK)
 
         xf_v = xf.rearrange("(p t) c -> p t c", t=PACK)
         tb_v = tb.rearrange("(p t) c -> p t c", t=PACK)
@@ -66,12 +66,12 @@ def tile_list_sum_steps_own_overtable_lagged_pl_kernel(
         nc.sync.dma_start(offs_t[:], offs)
         fk_t = tile("fk_t", [P, PACK], F32)
         nc.sync.dma_start(out=fk_t[:], in_=fk.rearrange("(p t) o -> p (t o)", t=PACK))
-        staged = placed("staged", [P, 3 * C + J], U8, 4096)
+        staged = placed("staged", [P, 3072], U8, 3840)[:, 0 : 3 * C + J]
         planes = tile("planes", [P, 3 * C + J], U8)
         load_rows(nc.sync, staged[0:32, 3 * C :], sx_scales, J)
         for a, scales in enumerate((w2_scales, w_scales, wb_scales)):
             load_rows(nc.scalar, staged[0:32, a * C : (a + 1) * C], scales, C)
-        nc.vector.memset(staged[32:64, :].bitcast(I32), 0)
+        nc.gpsimd.memset(staged[32:64, :].bitcast(I32), 0)
         nc.vector.memset(staged[64:128, :].bitcast(I32), 0)
         x01 = tile("x01", [P, 2, C], F32)
         nc.sync.dma_start(out=x01[:], in_=xf_v[:, 0:2, :])
@@ -85,49 +85,51 @@ def tile_list_sum_steps_own_overtable_lagged_pl_kernel(
         nc.gpsimd.dma_start(out=sx_t[:].bitcast(I32), in_=sx_words[0].bitcast(I32))
         offs2_t = tile("offs2_t", [P, J // 16], U16)
         nc.sync.dma_start(offs2_t[:], offs2)
-        tb01 = tile("tb01", [P, 2, C], F32)
-        nc.sync.dma_start(out=tb01[:], in_=tb_v[:, 0:2, :])
 
         g = tile("g", [P, PACK, PAD + J], F32)
         zeros = tile("zeros", [P, PACK, 1], F32)
         nc.vector.memset(zeros[:], 0.0)
         nc.scalar.activation(g[:, :, PAD - 1 : PAD], zeros[:], COPY)
         nc.vector.tensor_copy(out=planes[:, 3 * C :].bitcast(I32), in_=staged[:, 3 * C :].bitcast(I32))
-        nc.vector.tensor_copy(out=planes[:, 0 : 3 * C].rearrange("p (a t m i) -> p a m t i", a=3, t=PACK, i=16),
-                              in_=staged[:, 0 : 3 * C].rearrange("p (a m i t) -> p a m t i", a=3, t=PACK, i=16))
+        nc.vector.tensor_copy(out=planes[:, 0 : 2 * C].rearrange("p (a t m i) -> p a m t i", a=2, t=PACK, i=16),
+                              in_=staged[:, 0 : 2 * C].rearrange("p (a m i t) -> p a m t i", a=2, t=PACK, i=16))
+        nc.vector.tensor_copy(out=planes[:, 2 * C : 3 * C].rearrange("p (t m i) -> p m t i", t=PACK, i=16),
+                              in_=staged[:, 2 * C : 3 * C].rearrange("p (m i t) -> p m t i", t=PACK, i=16))
         for q in range(1, 4):
             nc.sync.dma_start(out=planes[32 * q : 32 * q + 4, :].bitcast(I32), in_=planes[4 * q : 4 * q + 4, :].bitcast(I32))
-        tb2 = placed("tb2", [P, C], F32, 3072)
+        tb01 = placed("tb01", [P, 2, C], F32, 0)
+        nc.sync.dma_start(out=tb01[:], in_=tb_v[:, 0:2, :])
+        tb2 = placed("tb2", [P, C], F32, 4096)
         nc.sync.dma_start(out=tb2[:], in_=tb_v[:, 2, :])
-        tb3 = placed("tb3", [P, C], F32, 5120)
+        tb3 = placed("tb3", [P, C], F32, 6144)
         nc.sync.dma_start(out=tb3[:], in_=tb_v[:, 3, :])
         w2s, ws, wbs, sxs = planes[:, 0:C], planes[:, C : 2 * C], planes[:, 2 * C : 3 * C], planes[:, 3 * C :]
 
-        picked = [tile("picked%d" % t, [P, J], F32) for t in range(PACK)]
+        steps = tile("steps", [P, PACK, J], F32)
         for t, x in ((0, x01), (2, x23)):
-            nc.scalar.activation(picked[t][:], x[:, 0, :].indirect(offs_t[:]), COPY)
-            nc.scalar.activation(g[:, t, PAD:], picked[t][:], COPY, scale=fk_t[:, t : t + 1])
-            nc.vector.tensor_copy(picked[t + 1][:], x[:, 1, :].indirect(offs_t[:]))
-            nc.vector.tensor_scalar(g[:, t + 1, PAD:], picked[t + 1][:], fk_t[:, t + 1 : t + 2], None, MULT)
+            nc.scalar.activation(g[:, t, PAD:], x[:, 0, :].indirect(offs_t[:]), COPY)
+            nc.vector.tensor_copy(g[:, t + 1, PAD:], x[:, 1, :].indirect(offs_t[:]))
+            nc.vector.scalar_tensor_tensor(steps[:, t : t + 2, :], g[:, t : t + 2, PAD - 1 : PAD - 1 + J], -0.6,
+                                           g[:, t : t + 2, PAD:], MULT, ADD)
 
-        w2d = deal(nc.scalar.copy, "w2d", w2_raw, U32, U32)
+        w2d = deal(nc.scalar.copy, "w2d", w2_raw, U32, U32, 4)
         wb_raw = placed("wb_raw", [P, 2 * C], U8, 8192)
         nc.sync.dma_start(out=wb_raw[:].bitcast(I32), in_=wb_words[0].bitcast(I32))
-        wd = deal(nc.scalar.copy, "wd", w_raw, U32, U32)
+        wd = deal(nc.scalar.copy, "wd", w_raw, U32, U32, 4)
         rs_t = placed("rs_t", [P, PACK, J], F32, 10240)
         nc.sync.dma_start(out=rs_t[:], in_=rs.rearrange("(p t) j -> p t j", t=PACK))
 
         a_bank = [ps.tile([P, PACK, H], F32, name="a_bank%d" % h) for h in range(2)]
         p_bank = [ps.tile([P, PACK, H], F32, name="p_bank%d" % h) for h in range(2)]
-        ub = [tile("ub%d" % h, [P, H, PACK], BF16) for h in range(2)]
+        fk_walk = fk_t[:].unsqueeze(1).unsqueeze(3).broadcast_to([P, H // 2, PACK, 2])
+        tg = tile("tg", [P, PACK, J], F32)
+        ub = [tile("ub0", [P, H * PACK], BF16), tg[:].rearrange("p t c -> p (t c)")[:, 2 * J + H : 3 * J + H].bitcast(BF16)]
         uq = [tile("uq%d" % h, [P, H], U32) for h in range(2)]
         us = [tile("us%d" % h, [P, H], U8) for h in range(2)]
         for h in range(2):
-            now = g[:, :, PAD + h * H : PAD + (h + 1) * H].rearrange("p t c -> p c t")
-            before = g[:, :, PAD - 1 + h * H : PAD - 1 + (h + 1) * H].rearrange("p t c -> p c t")
-            nc.vector.scalar_tensor_tensor(ub[h][:], before, -0.6, now, MULT, ADD)
+            nc.vector.tensor_tensor(walk_words(ub[h][:]), walk_planes(steps[:, :, h * H : (h + 1) * H]), fk_walk, MULT)
         for h in range(2):
-            nc.vector.quantize_mx(out=uq[h][:].bitcast(E4M3), scales=us[h][:], in_=ub[h][:].rearrange("p c t -> p (c t)"))
+            nc.vector.quantize_mx(out=uq[h][:].bitcast(E4M3), scales=us[h][:], in_=ub[h][:])
         for h in range(2):
             for t in range(PACK):
                 nc.tensor.matmul_mx(out=a_bank[h][:, t, :], lhsT=w2d[:, t * P : (t + 1) * P].bitcast(E5M2),
@@ -139,13 +141,13 @@ def tile_list_sum_steps_own_overtable_lagged_pl_kernel(
                                     lhsT_scale=ws[:, t * P : (t + 1) * P], rhs=uq[h][:].bitcast(E4M3),
                                     rhs_scale=us[h][:], start=False, stop=(t == PACK - 1))
 
-        tg = tile("tg", [P, PACK, J], F32)
         nc.scalar.activation(tg[:, 0, :], tb01[:, 0, :].indirect(offs2_t[:]), COPY)
-        nc.vector.tensor_copy(tg[:, 1, :], tb01[:, 1, :].indirect(offs2_t[:]))
-        nc.scalar.activation(tg[:, 2, :], tb2[:].indirect(offs2_t[:]), COPY)
+        nc.scalar.activation(tg[:, 1, :], tb01[:, 1, :].indirect(offs2_t[:]), COPY)
+        nc.scalar.activation(tg[:, 2, 0:H], tb2[:].indirect(offs2_t[:, 0:8]), COPY)
+        nc.vector.tensor_copy(tg[:, 2, H:J], tb2[:].indirect(offs2_t[:, 8:16]))
         nc.vector.tensor_copy(tg[:, 3, 0:H], tb3[:].indirect(offs2_t[:, 0:8]))
         nc.scalar.activation(tg[:, 3, H:J], tb3[:].indirect(offs2_t[:, 8:16]), COPY)
-        wbd = deal(nc.scalar.copy, "wbd", wb_raw, U8, U16)
+        wbd = deal(nc.scalar.copy, "wbd", wb_raw, U8, U16, 8)
 
         db = [tile("db%d" % h, [P, H * PACK], BF16) for h in range(2)]
         hb = [tile("hb%d" % h, [P, H * PACK], BF16) for h in range(2)]

@@ -44,7 +44,7 @@ def tile_list_sum_steps_own_overtable_lagged_pl_kernel(
             return held.tile(shape, dtype, name=name, offset=offset, align_bytes=64)
 
         def load_rows(queue, dst, scales, width):
-            rows = scales[0].bitcast(I32).unsqueeze(0).broadcast_to([2, 16, width // 4])
+            rows = scales[0].bitcast(I32).unsqueeze(1).broadcast_to([16, 2, width // 4])
             queue.dma_start(out=dst.bitcast(I32), in_=rows)
 
         def deal(copy, name, raw, dtype, view, run):
@@ -64,15 +64,21 @@ def tile_list_sum_steps_own_overtable_lagged_pl_kernel(
 
         offs_t = tile("offs_t", [P, J // 16], U16)
         nc.sync.dma_start(offs_t[:], offs)
-        fk_t = tile("fk_t", [P, PACK], F32)
-        nc.sync.dma_start(out=fk_t[:], in_=fk.rearrange("(p t) o -> p (t o)", t=PACK))
+        offs2_t = tile("offs2_t", [P, J // 16], U16)
+        nc.sync.dma_start(offs2_t[:], offs2)
         staged = placed("staged", [P, 3072], U8, 3840)[:, 0 : 3 * C + J]
         planes = tile("planes", [P, 3 * C + J], U8)
         load_rows(nc.sync, staged[0:32, 3 * C :], sx_scales, J)
         for a, scales in enumerate((w2_scales, w_scales, wb_scales)):
             load_rows(nc.scalar, staged[0:32, a * C : (a + 1) * C], scales, C)
-        nc.gpsimd.memset(staged[32:64, :].bitcast(I32), 0)
+        g = tile("g", [P, PACK, PAD + J], F32)
+        zeros = tile("zeros", [P, PACK, 1], F32)
+        nc.vector.memset(zeros[:], 0.0)
+        nc.scalar.activation(g[:, :, PAD - 1 : PAD], zeros[:], COPY)
+        dealt_rows = tile("dealt_rows", [P, 3 * C + J], U8)
+        nc.vector.memset(staged[32:64, :].bitcast(I32), 0)
         nc.vector.memset(staged[64:128, :].bitcast(I32), 0)
+        nc.vector.memset(planes[:].bitcast(I32), 0)
         x01 = tile("x01", [P, 2, C], F32)
         nc.sync.dma_start(out=x01[:], in_=xf_v[:, 0:2, :])
         x23 = tile("x23", [P, 2, C], F32)
@@ -81,22 +87,18 @@ def tile_list_sum_steps_own_overtable_lagged_pl_kernel(
         nc.sync.dma_start(out=w2_raw[:].bitcast(I32), in_=w2_words[0].rearrange("p n t -> p (n t)").bitcast(I32))
         w_raw = placed("w_raw", [P, C], U32, 10240)
         nc.sync.dma_start(out=w_raw[:].bitcast(I32), in_=w_words[0].rearrange("p n t -> p (n t)").bitcast(I32))
+        fk_t = tile("fk_t", [P, PACK], F32)
+        nc.gpsimd.dma_start(out=fk_t[:], in_=fk.rearrange("(p t) o -> p (t o)", t=PACK))
         sx_t = tile("sx_t", [P, 2 * J], U8)
         nc.gpsimd.dma_start(out=sx_t[:].bitcast(I32), in_=sx_words[0].bitcast(I32))
-        offs2_t = tile("offs2_t", [P, J // 16], U16)
-        nc.sync.dma_start(offs2_t[:], offs2)
 
-        g = tile("g", [P, PACK, PAD + J], F32)
-        zeros = tile("zeros", [P, PACK, 1], F32)
-        nc.vector.memset(zeros[:], 0.0)
-        nc.scalar.activation(g[:, :, PAD - 1 : PAD], zeros[:], COPY)
-        nc.vector.tensor_copy(out=planes[:, 3 * C :].bitcast(I32), in_=staged[:, 3 * C :].bitcast(I32))
-        nc.vector.tensor_copy(out=planes[:, 0 : 2 * C].rearrange("p (a t m i) -> p a m t i", a=2, t=PACK, i=16),
+        nc.vector.tensor_copy(out=dealt_rows[:, 3 * C :].bitcast(I32), in_=staged[:, 3 * C :].bitcast(I32))
+        nc.vector.tensor_copy(out=dealt_rows[:, 0 : 2 * C].rearrange("p (a t m i) -> p a m t i", a=2, t=PACK, i=16),
                               in_=staged[:, 0 : 2 * C].rearrange("p (a m i t) -> p a m t i", a=2, t=PACK, i=16))
-        nc.vector.tensor_copy(out=planes[:, 2 * C : 3 * C].rearrange("p (t m i) -> p m t i", t=PACK, i=16),
+        nc.vector.tensor_copy(out=dealt_rows[:, 2 * C : 3 * C].rearrange("p (t m i) -> p m t i", t=PACK, i=16),
                               in_=staged[:, 2 * C : 3 * C].rearrange("p (m i t) -> p m t i", t=PACK, i=16))
-        for q in range(1, 4):
-            nc.sync.dma_start(out=planes[32 * q : 32 * q + 4, :].bitcast(I32), in_=planes[4 * q : 4 * q + 4, :].bitcast(I32))
+        for q in range(4):
+            nc.sync.dma_start(out=planes[32 * q : 32 * q + 4, :].bitcast(I32), in_=dealt_rows[8 * q : 8 * q + 8 : 2, :].bitcast(I32))
         tb01 = placed("tb01", [P, 2, C], F32, 0)
         nc.sync.dma_start(out=tb01[:], in_=tb_v[:, 0:2, :])
         tb2 = placed("tb2", [P, C], F32, 4096)

@@ -66,7 +66,7 @@ def tile_list_sum_steps_own_overtable_lagged_pl_kernel(
         nc.sync.dma_start(offs_t[:], offs)
         offs2_t = tile("offs2_t", [P, J // 16], U16)
         nc.sync.dma_start(offs2_t[:], offs2)
-        staged = placed("staged", [P, 3072], U8, 3840)[:, 0 : 3 * C + J]
+        staged = placed("staged", [P, 4608], U8, 1792)[:, 0 : 3 * C + J]
         planes = tile("planes", [P, 3 * C + J], U8)
         load_rows(nc.sync, staged[0:32, 3 * C :], sx_scales, J)
         for a, scales in enumerate((w2_scales, w_scales, wb_scales)):
@@ -99,12 +99,9 @@ def tile_list_sum_steps_own_overtable_lagged_pl_kernel(
                               in_=staged[:, 2 * C : 3 * C].rearrange("p (m i t) -> p m t i", t=PACK, i=16))
         for q in range(4):
             nc.sync.dma_start(out=planes[32 * q : 32 * q + 4, :].bitcast(I32), in_=dealt_rows[8 * q : 8 * q + 8 : 2, :].bitcast(I32))
-        tb01 = placed("tb01", [P, 2, C], F32, 0)
-        nc.sync.dma_start(out=tb01[:], in_=tb_v[:, 0:2, :])
-        tb2 = placed("tb2", [P, C], F32, 4096)
-        nc.sync.dma_start(out=tb2[:], in_=tb_v[:, 2, :])
-        tb3 = placed("tb3", [P, C], F32, 6144)
-        nc.sync.dma_start(out=tb3[:], in_=tb_v[:, 3, :])
+        tb_t = [placed("tb%d" % t, [P, C], F32, 2048 * t) for t in range(PACK)]
+        for t in range(PACK):
+            nc.sync.dma_start(out=tb_t[t][:], in_=tb_v[:, t, :])
         w2s, ws, wbs, sxs = planes[:, 0:C], planes[:, C : 2 * C], planes[:, 2 * C : 3 * C], planes[:, 3 * C :]
 
         steps = tile("steps", [P, PACK, J], F32)
@@ -125,7 +122,7 @@ def tile_list_sum_steps_own_overtable_lagged_pl_kernel(
         p_bank = [ps.tile([P, PACK, H], F32, name="p_bank%d" % h) for h in range(2)]
         fk_walk = fk_t[:].unsqueeze(1).unsqueeze(3).broadcast_to([P, H // 2, PACK, 2])
         tg = tile("tg", [P, PACK, J], F32)
-        ub = [tile("ub0", [P, H * PACK], BF16), tg[:].rearrange("p t c -> p (t c)")[:, 2 * J + H : 3 * J + H].bitcast(BF16)]
+        ub = [tile("ub0", [P, H * PACK], BF16), tg[:].rearrange("p t c -> p (t c)")[:, 3 * J : 4 * J].bitcast(BF16)]
         uq = [tile("uq%d" % h, [P, H], U32) for h in range(2)]
         us = [tile("us%d" % h, [P, H], U8) for h in range(2)]
         for h in range(2):
@@ -143,12 +140,10 @@ def tile_list_sum_steps_own_overtable_lagged_pl_kernel(
                                     lhsT_scale=ws[:, t * P : (t + 1) * P], rhs=uq[h][:].bitcast(E4M3),
                                     rhs_scale=us[h][:], start=False, stop=(t == PACK - 1))
 
-        nc.scalar.activation(tg[:, 0, :], tb01[:, 0, :].indirect(offs2_t[:]), COPY)
-        nc.scalar.activation(tg[:, 1, :], tb01[:, 1, :].indirect(offs2_t[:]), COPY)
-        nc.scalar.activation(tg[:, 2, 0:H], tb2[:].indirect(offs2_t[:, 0:8]), COPY)
-        nc.vector.tensor_copy(tg[:, 2, H:J], tb2[:].indirect(offs2_t[:, 8:16]))
-        nc.vector.tensor_copy(tg[:, 3, 0:H], tb3[:].indirect(offs2_t[:, 0:8]))
-        nc.scalar.activation(tg[:, 3, H:J], tb3[:].indirect(offs2_t[:, 8:16]), COPY)
+        for t in range(3):
+            nc.scalar.activation(tg[:, t, :], tb_t[t][:].indirect(offs2_t[:]), COPY)
+        nc.vector.tensor_copy(tg[:, 3, 0:H], tb_t[3][:].indirect(offs2_t[:, 0:8]))
+        nc.scalar.activation(tg[:, 3, H:J], tb_t[3][:].indirect(offs2_t[:, 8:16]), COPY)
         wbd = deal(nc.scalar.copy, "wbd", wb_raw, U8, U16, 8)
 
         db = [tile("db%d" % h, [P, H * PACK], BF16) for h in range(2)]
@@ -184,10 +179,11 @@ def tile_list_sum_steps_own_overtable_lagged_pl_kernel(
             nc.vector.scalar_tensor_tensor(y[h][:], lag[:, :, h * H : (h + 1) * H], -0.7, p_bank[h][:], MULT, ADD)
             nc.sync.dma_start(out=out_v[:, :, h * H : (h + 1) * H], in_=y[h][:])
         nc.scalar.copy(out=walk_words(yb[0][:]), in_=walk_planes(y[0][:]))
-        nc.vector.tensor_copy(out=walk_words(yb[1][:]), in_=walk_planes(y[1][:]))
+        nc.vector.tensor_copy(out=walk_words(yb[1][:, 0 : 2 * H]), in_=walk_planes(y[1][:, :, 0 : H // 2]))
+        nc.scalar.copy(out=walk_words(yb[1][:, 2 * H :]), in_=walk_planes(y[1][:, :, H // 2 :]))
         for h in range(2):
             nc.vector.quantize_mx(out=yq[h][:].bitcast(E4M3), scales=ys[:, h * H : (h + 1) * H], in_=yb[h][:])
-            nc.sync.dma_start(out=words_v[:, h * H : (h + 1) * H], in_=yq[h][:].bitcast(I32))
+            (nc.scalar if h else nc.sync).dma_start(out=words_v[:, h * H : (h + 1) * H], in_=yq[h][:].bitcast(I32))
         for q in range(4):
-            queue = nc.scalar if q % 2 else nc.sync
+            queue = nc.scalar if q == 3 else nc.sync
             queue.dma_start(out=out_2[0].bitcast(I32)[4 * q : 4 * q + 4, :], in_=ys[32 * q : 32 * q + 4, :].bitcast(I32))

from contextlib import ExitStack

import concourse.mybir as mybir

F32 = mybir.dt.float32
BF16 = mybir.dt.bfloat16
I32 = mybir.dt.int32
U32 = mybir.dt.uint32
U16 = mybir.dt.uint16
U8 = mybir.dt.uint8
E4M3 = mybir.dt.float8_e4m3fn_x4
E5M2 = mybir.dt.float8_e5m2_x4
E2M1 = mybir.dt.float4_e2m1fn_x4
MULT = mybir.AluOpType.mult
ADD = mybir.AluOpType.add
SUB = mybir.AluOpType.subtract
MAX = mybir.AluOpType.max
COPY = mybir.ActivationFunctionType.Copy

RELU = mybir.ActivationFunctionType.Relu
P = 128
PACK = 4
C = 512
J = 256
H = 128
PAD = 8
FLOPS = 3 * 2 * 512 * 512 * 256


def tile_list_sum_steps_own_overtable_lagged_pl_kernel(
    tc, xf, fk, w_words, w_scales, sx_words, sx_scales, w2_words, w2_scales, tb, wb_words, wb_scales, rs, offs, offs2,
    out_0, out_1, out_2,
):
    nc = tc.nc
    with ExitStack() as ctx:
        sb = ctx.enter_context(tc.tile_pool(name="sb", bufs=1))
        held = ctx.enter_context(tc.tile_pool(name="held", bufs=1))
        ps = ctx.enter_context(tc.psum_pool(name="ps", bufs=1))

        def tile(name, shape, dtype):
            return sb.tile(shape, dtype, name=name, align_bytes=64)

        def placed(name, shape, dtype, offset):
            return held.tile(shape, dtype, name=name, offset=offset, align_bytes=64)

        def load_rows(queue, dst, scales, width):
            rows = scales[0].bitcast(I32).unsqueeze(1).broadcast_to([16, 2, width // 4])
            queue.dma_start(out=dst.bitcast(I32), in_=rows)

        def deal(copy, name, raw, dtype, view, run):
            dealt = tile(name, raw.shape, dtype)
            copy(out=dealt[:].bitcast(view).rearrange("p (t m i) -> p m t i", t=PACK, i=run),
                 in_=raw[:].bitcast(view).rearrange("p (m i t) -> p m t i", t=PACK, i=run))
            return dealt

        def walk_planes(ap):
            return ap.rearrange("p t (c i) -> p c t i", i=2)

        def walk_words(ap):
            return ap.rearrange("p (c i t) -> p c t i", i=2, t=PACK)

        xf_v = xf.rearrange("(p t) c -> p t c", t=PACK)
        tb_v = tb.rearrange("(p t) c -> p t c", t=PACK)

        offs_t = tile("offs_t", [P, J // 16], U16)
        nc.sync.dma_start(offs_t[:], offs)
        offs2_t = tile("offs2_t", [P, J // 16], U16)
        nc.sync.dma_start(offs2_t[:], offs2)
        staged = placed("staged", [P, 4608], U8, 1792)[:, 0 : 3 * C + J]
        planes = tile("planes", [P, 3 * C + J], U8)
        load_rows(nc.sync, staged[0:32, 3 * C :], sx_scales, J)
        for a, scales in enumerate((w2_scales, w_scales, wb_scales)):
            load_rows(nc.scalar, staged[0:32, a * C : (a + 1) * C], scales, C)
        g = tile("g", [P, PACK, PAD + J], F32)
        zeros = tile("zeros", [P, PACK, 1], F32)
        nc.vector.memset(zeros[:], 0.0)
        nc.scalar.activation(g[:, :, PAD - 1 : PAD], zeros[:], COPY)
        dealt_rows = tile("dealt_rows", [P, 3 * C + J], U8)
        nc.vector.memset(staged[32:64, :].bitcast(I32), 0)
        nc.vector.memset(staged[64:128, :].bitcast(I32), 0)
        nc.vector.memset(planes[:].bitcast(I32), 0)
        x01 = tile("x01", [P, 2, C], F32)
        nc.sync.dma_start(out=x01[:], in_=xf_v[:, 0:2, :])
        x23 = tile("x23", [P, 2, C], F32)
        nc.sync.dma_start(out=x23[:], in_=xf_v[:, 2:4, :])
        w2_raw = placed("w2_raw", [P, C], U32, 8192)
        nc.sync.dma_start(out=w2_raw[:].bitcast(I32), in_=w2_words[0].rearrange("p n t -> p (n t)").bitcast(I32))
        w_raw = placed("w_raw", [P, C], U32, 10240)
        nc.sync.dma_start(out=w_raw[:].bitcast(I32), in_=w_words[0].rearrange("p n t -> p (n t)").bitcast(I32))
        fk_t = tile("fk_t", [P, PACK], F32)
        nc.gpsimd.dma_start(out=fk_t[:], in_=fk.rearrange("(p t) o -> p (t o)", t=PACK))
        sx_t = tile("sx_t", [P, 2 * J], U8)
        nc.gpsimd.dma_start(out=sx_t[:].bitcast(I32), in_=sx_words[0].bitcast(I32))

        nc.vector.tensor_copy(out=dealt_rows[:, 3 * C :].bitcast(I32), in_=staged[:, 3 * C :].bitcast(I32))
        nc.vector.tensor_copy(out=dealt_rows[:, 0 : 2 * C].rearrange("p (a t m i) -> p a m t i", a=2, t=PACK, i=16),
                              in_=staged[:, 0 : 2 * C].rearrange("p (a m i t) -> p a m t i", a=2, t=PACK, i=16))
        nc.vector.tensor_copy(out=dealt_rows[:, 2 * C : 3 * C].rearrange("p (t m i) -> p m t i", t=PACK, i=16),
                              in_=staged[:, 2 * C : 3 * C].rearrange("p (m i t) -> p m t i", t=PACK, i=16))
        for q in range(4):
            nc.sync.dma_start(out=planes[32 * q : 32 * q + 4, :].bitcast(I32), in_=dealt_rows[8 * q : 8 * q + 8 : 2, :].bitcast(I32))
        tb_t = [placed("tb%d" % t, [P, C], F32, 2048 * t) for t in range(PACK)]
        for t in range(PACK):
            nc.sync.dma_start(out=tb_t[t][:], in_=tb_v[:, t, :])
        w2s, ws, wbs, sxs = planes[:, 0:C], planes[:, C : 2 * C], planes[:, 2 * C : 3 * C], planes[:, 3 * C :]

        steps = tile("steps", [P, PACK, J], F32)
        for t, x in ((0, x01), (2, x23)):
            nc.scalar.activation(g[:, t, PAD:], x[:, 0, :].indirect(offs_t[:]), COPY)
            nc.vector.tensor_copy(g[:, t + 1, PAD:], x[:, 1, :].indirect(offs_t[:]))
            nc.vector.scalar_tensor_tensor(steps[:, t : t + 2, :], g[:, t : t + 2, PAD - 1 : PAD - 1 + J], -0.6,
                                           g[:, t : t + 2, PAD:], MULT, ADD)

        w2d = deal(nc.scalar.copy, "w2d", w2_raw, U32, U32, 4)
        wb_raw = placed("wb_raw", [P, 2 * C], U8, 8192)
        nc.sync.dma_start(out=wb_raw[:].bitcast(I32), in_=wb_words[0].bitcast(I32))
        wd = deal(nc.scalar.copy, "wd", w_raw, U32, U32, 4)
        rs_t = placed("rs_t", [P, PACK, J], F32, 10240)
        nc.sync.dma_start(out=rs_t[:], in_=rs.rearrange("(p t) j -> p t j", t=PACK))

        a_bank = [ps.tile([P, PACK, H], F32, name="a_bank%d" % h) for h in range(2)]
        p_bank = [ps.tile([P, PACK, H], F32, name="p_bank%d" % h) for h in range(2)]
        fk_walk = fk_t[:].unsqueeze(1).unsqueeze(3).broadcast_to([P, H // 2, PACK, 2])
        tg = tile("tg", [P, PACK, J], F32)
        ub = [tile("ub0", [P, H * PACK], BF16), tg[:].rearrange("p t c -> p (t c)")[:, 3 * J : 4 * J].bitcast(BF16)]
        uq = [tile("uq%d" % h, [P, H], U32) for h in range(2)]
        us = [tile("us%d" % h, [P, H], U8) for h in range(2)]
        for h in range(2):
            nc.vector.tensor_tensor(walk_words(ub[h][:]), walk_planes(steps[:, :, h * H : (h + 1) * H]), fk_walk, MULT)
        for h in range(2):
            nc.vector.quantize_mx(out=uq[h][:].bitcast(E4M3), scales=us[h][:], in_=ub[h][:])
        for h in range(2):
            for t in range(PACK):
                nc.tensor.matmul_mx(out=a_bank[h][:, t, :], lhsT=w2d[:, t * P : (t + 1) * P].bitcast(E5M2),
                                    lhsT_scale=w2s[:, t * P : (t + 1) * P],
                                    rhs=sx_t[:, 2 * h * H : 2 * (h + 1) * H].bitcast(E2M1),
                                    rhs_scale=sxs[:, h * H : (h + 1) * H], start=(t == 0), stop=False)
            for t in range(PACK):
                nc.tensor.matmul_mx(out=a_bank[h][:, t, :], lhsT=wd[:, t * P : (t + 1) * P].bitcast(E4M3),
                                    lhsT_scale=ws[:, t * P : (t + 1) * P], rhs=uq[h][:].bitcast(E4M3),
                                    rhs_scale=us[h][:], start=False, stop=(t == PACK - 1))

        for t in range(3):
            nc.scalar.activation(tg[:, t, :], tb_t[t][:].indirect(offs2_t[:]), COPY)
        nc.vector.tensor_copy(tg[:, 3, 0:H], tb_t[3][:].indirect(offs2_t[:, 0:8]))
        nc.scalar.activation(tg[:, 3, H:J], tb_t[3][:].indirect(offs2_t[:, 8:16]), COPY)
        wbd = deal(nc.scalar.copy, "wbd", wb_raw, U8, U16, 8)

        db = [tile("db%d" % h, [P, H * PACK], BF16) for h in range(2)]
        hb = [tile("hb%d" % h, [P, H * PACK], BF16) for h in range(2)]
        hq = [tile("hq%d" % h, [P, H], U32) for h in range(2)]
        hs = [tile("hs%d" % h, [P, H], U8) for h in range(2)]
        for h in range(2):
            nc.vector.tensor_tensor(walk_words(db[h][:]), walk_planes(a_bank[h][:]), walk_planes(tg[:, :, h * H : (h + 1) * H]), SUB)
        nc.scalar.activation(hb[0][:], db[0][:], RELU)
        nc.vector.tensor_scalar(hb[1][:], db[1][:], 0.0, None, MAX)
        for h in range(2):
            nc.vector.quantize_mx(out=hq[h][:].bitcast(E5M2), scales=hs[h][:], in_=hb[h][:])
        for h in range(2):
            for t in range(PACK):
                nc.tensor.matmul_mx(out=p_bank[h][:, t, :], lhsT=wbd[:, 2 * t * P : 2 * (t + 1) * P].bitcast(E2M1),
                                    lhsT_scale=wbs[:, t * P : (t + 1) * P], rhs=hq[h][:].bitcast(E5M2),
                                    rhs_scale=hs[h][:], start=True, stop=True)

        lag = tile("lag", [P, PACK, J], F32)
        ratio = 0.5 / -0.7
        nc.vector.tensor_scalar(lag[:, :, 0:1], rs_t[:, :, 0:1], ratio, None, MULT)
        y = [tile("y%d" % h, [P, PACK, H], F32) for h in range(2)]
        yb = [tile("yb%d" % h, [P, H * PACK], BF16) for h in range(2)]
        yq = [tile("yq%d" % h, [P, H], U32) for h in range(2)]
        ys = tile("ys", [P, J], U8)
        out_v = out_0.rearrange("(p t) j -> p t j", t=PACK)
        words_v = out_1[0].rearrange("p c t -> p (c t)").bitcast(I32)
        for h in range(2):
            n = min(H, J - 1 - h * H)
            cols = slice(h * H + 1, h * H + 1 + n)
            nc.vector.scalar_tensor_tensor(lag[:, :, cols], rs_t[:, :, cols], ratio, p_bank[h][:, :, 0:n], MULT, ADD)
        for h in range(2):
            nc.vector.scalar_tensor_tensor(y[h][:], lag[:, :, h * H : (h + 1) * H], -0.7, p_bank[h][:], MULT, ADD)
            nc.sync.dma_start(out=out_v[:, :, h * H : (h + 1) * H], in_=y[h][:])
        nc.scalar.copy(out=walk_words(yb[0][:]), in_=walk_planes(y[0][:]))
        nc.vector.tensor_copy(out=walk_words(yb[1][:, 0 : 2 * H]), in_=walk_planes(y[1][:, :, 0 : H // 2]))
        nc.scalar.copy(out=walk_words(yb[1][:, 2 * H :]), in_=walk_planes(y[1][:, :, H // 2 :]))
        for h in range(2):
            nc.vector.quantize_mx(out=yq[h][:].bitcast(E4M3), scales=ys[:, h * H : (h + 1) * H], in_=yb[h][:])
            (nc.scalar if h else nc.sync).dma_start(out=words_v[:, h * H : (h + 1) * H], in_=yq[h][:].bitcast(I32))
        for q in range(4):
            queue = nc.scalar if q == 3 else nc.sync
            queue.dma_start(out=out_2[0].bitcast(I32)[4 * q : 4 * q + 4, :], in_=ys[32 * q : 32 * q + 4, :].bitcast(I32))
